import numpy as np
import ml_dtypes


def mxq(x, axis, fmt="e4m3"):
    dtype, down = {"e4m3": (ml_dtypes.float8_e4m3fn, 7), "e5m2": (ml_dtypes.float8_e5m2, 14)}[fmt]
    v = np.moveaxis(np.asarray(x, np.float32).astype(ml_dtypes.bfloat16).astype(np.float64), axis, -1)
    blocks = v.reshape(v.shape[:-1] + (-1, 32))
    amax = np.abs(blocks).max(-1, keepdims=True)
    byte = np.maximum(np.where(amax > 0, np.frexp(amax)[1] - 1 + 127, 0) - down, 1)
    scale = np.exp2(byte - 127.0)
    codes = (blocks / scale).astype(np.float32).astype(dtype).astype(np.float64)
    return np.moveaxis((codes * scale).reshape(v.shape), -1, axis)


WIDE = False


def mx_kscale(k):
    if not WIDE:
        return np.ones(k)
    levels = np.array([10, -10, 5, -5, 0])
    if k % 512:
        return np.exp2(np.random.permutation(np.resize(levels, k // 32))).repeat(32)
    a = np.empty((k // 512, 16))
    for p in range(k // 512):
        a[p, :8] = np.random.permutation(np.resize(levels, 8))
        for g in range(8):
            far = levels[np.abs(levels - a[p, g]) >= 10]
            a[p, g + 8] = far[np.random.randint(len(far))]
    return np.exp2(a.ravel()).repeat(32)


def f64(x):
    return np.asarray(x).astype(np.float64)


def striped8(idx):
    return np.asarray(idx).reshape(8, -1, 16).transpose(0, 2, 1).reshape(128, -1).astype(np.uint16)


def unstriped8(offs):
    return offs.reshape(8, 16, -1).transpose(0, 2, 1).reshape(8, -1).astype(np.int64)


def pick8(x, idx, run):
    r = np.arange(len(x))
    return x[r[:, None], idx[r % (8 * run) // run]]


E2M1 = np.array([0.0, 0.5, 1.0, 1.5, 2.0, 3.0, 4.0, 6.0, -0.0, -0.5, -1.0, -1.5, -2.0, -3.0, -4.0, -6.0])


def pack_weight(w, fmt):
    k, n = w.shape
    w = f64(np.asarray(w, np.float32).astype(ml_dtypes.bfloat16)).reshape(k // 32, 32, n)
    amax = np.abs(w).max(1)
    if fmt == "e4m3":
        byte = np.frexp(amax)[1] - 1 + 127 - 7
    else:
        mant, ex = np.frexp(amax / 6.0)
        byte = np.where(mant > 0.5, ex, ex - 1) + 127
    byte = np.clip(np.where(amax > 0, byte, 1), 1, 254)
    scaled = (w * np.exp2(127.0 - byte)[:, None, :]).reshape(k, n).astype(np.float32)
    by_word = np.ascontiguousarray(scaled.reshape(k // 512, 128, 4, n).transpose(0, 1, 3, 2))
    if fmt == "e4m3":
        words = by_word.astype(ml_dtypes.float8_e4m3fn).view(np.uint8)
    else:
        c = by_word.astype(ml_dtypes.float4_e2m1fn).view(np.uint8) & 0xF
        words = (c[..., 0::2] | (c[..., 1::2] << 4)).reshape(k // 512, 128, 2 * n)
    return np.ascontiguousarray(words), np.ascontiguousarray(byte.astype(np.uint8).reshape(k // 512, 16, n))


def unpack_weight(words, scales, fmt):
    g, _, n = scales.shape
    words = np.ascontiguousarray(words).reshape(g, 128, n, -1)
    if fmt == "e4m3":
        vals = words.view(ml_dtypes.float8_e4m3fn).astype(np.float64)
    else:
        nib = np.empty((g, 128, n, 4), np.uint8)
        nib[..., 0::2] = words & 0xF
        nib[..., 1::2] = words >> 4
        vals = E2M1[nib]
    vals = vals * np.repeat(np.exp2(scales.astype(np.float64) - 127.0), 8, axis=1)[..., None]
    return vals.transpose(0, 1, 3, 2).reshape(g * 512, n)


D, T, I, Q = 512, 1024, 512, 128


def setup_inputs():
    n = np.random.standard_normal
    idx = np.stack([np.random.permutation(T)[:I] for _ in range(8)])
    idx2 = np.stack([np.random.permutation(T)[:I] for _ in range(8)])
    idx3 = np.stack([np.random.permutation(T)[:I] for _ in range(8)])
    idx4 = np.stack([np.random.permutation(T)[:I] for _ in range(8)])
    fd = mx_kscale(D)
    keysp = pack_weight(n((D, T)) / fd[:, None], "e2m1")
    return {
        "query": (n((D, Q)) * 0.9 / np.sqrt(D) * fd[:, None]).astype(np.float32),
        "query2": (n((D, Q)) * 0.9 / np.sqrt(D) * fd[:, None]).astype(np.float32),
        "keys_words": keysp[0],
        "keys_scales": keysp[1],
        "lam": (np.random.uniform(1.0, 2.5, (Q, 1))).astype(np.float32),
        "damp": (np.random.uniform(1.0, 4.0, (Q, 1))).astype(np.float32),
        "old": (np.random.uniform(0.0, 2.0, (Q, T))).astype(np.float32),
        "gainm": (np.random.uniform(0.5, 1.5, (Q, I))).astype(np.float32),
        "offs": striped8(idx),
        "offs2": striped8(idx2),
        "offs3": striped8(idx3),
        "offs4": striped8(idx4),
    }


def reference(query, query2, keys_words, keys_scales, lam, damp, old, gainm, offs, offs2, offs3, offs4):
    idx = unstriped8(offs)
    idx2 = unstriped8(offs2)
    idx3 = unstriped8(offs3)
    idx4 = unstriped8(offs4)
    keysu = unpack_weight(keys_words, keys_scales, "e2m1")
    queryq = mxq(f64(query), 0, "e4m3")
    a = queryq.T @ keysu
    query2q = mxq(f64(query2), 0, "e4m3")
    b = query2q.T @ keysu
    e1s = np.exp(pick8(a, idx, 16))
    s = e1s / (e1s + np.exp(pick8(a, idx2, 16)) + np.exp(pick8(b, idx3, 16))) * f64(lam)
    p = np.exp(s - np.max(s, axis=1, keepdims=True))
    r = p / np.sum(p, axis=1, keepdims=True) * 512.0
    u0 = np.log(r * f64(damp) + 1.0)
    w = u0 / np.sum(u0, axis=1, keepdims=True)
    ws = w * f64(gainm) * 512.0
    wf = np.zeros((Q, T))
    wf[np.arange(Q)[:, None], idx4[np.arange(Q) % 128 // 16]] = ws
    y = f64(old) + wf
    return y

@@ -1,0 +1,201 @@
+from contextlib import ExitStack
+
+import concourse.mybir as mybir
+
+D, T, I, Q = 512, 1024, 512, 128
+FLOPS = 2 * 2 * D * T * Q
+
+F32 = mybir.dt.float32
+BF16 = mybir.dt.bfloat16
+I32 = mybir.dt.int32
+U32 = mybir.dt.uint32
+U16 = mybir.dt.uint16
+U8 = mybir.dt.uint8
+FP8X4 = mybir.dt.float8_e4m3fn_x4
+FP4X4 = mybir.dt.float4_e2m1fn_x4
+ALU = mybir.AluOpType
+ACT = mybir.ActivationFunctionType
+
+P = 128
+PACK = 4
+BANK = 512
+HALF = I // 2
+LCOL = HALF // 16
+CAP = float(2 ** 30)
+
+
+def tile_attend_quotaratio_dampened_moved_heads_kernel(
+    tc, query, query2, keys_words, keys_scales, lam, damp, old, gainm, offs, offs2, offs3, offs4, out
+):
+    nc = tc.nc
+    with ExitStack() as ctx:
+        keep = ctx.enter_context(tc.tile_pool(name="keep", bufs=1))
+        psum = ctx.enter_context(tc.psum_pool(name="psum", bufs=1))
+
+        def sb(name, shape, dtype=F32):
+            return keep.tile(shape, dtype, name=name, align_bytes=64)
+
+        key_scales = sb("key_scales", [P, T], U8)
+        nc.vector.memset(key_scales[:].bitcast(I32), 0)
+        for g in range(4):
+            nc.scalar.dma_start(
+                out=key_scales[32 * g : 32 * g + 4, :].bitcast(I32), in_=keys_scales[0, 4 * g : 4 * g + 4, :].bitcast(I32)
+            )
+        q_raw = [sb("q_raw%d" % j, [P, PACK, Q]) for j in range(2)]
+        key_words = sb("key_words", [P, 2 * T], U8)
+        lists = [keep.tile([P, I // 16], U16, name="list%d" % j) for j in range(4)]
+        nc.sync.dma_start(out=q_raw[0][:], in_=query.rearrange("(p j) w -> p j w", j=PACK))
+        nc.sync.dma_start(out=key_words[:].bitcast(I32), in_=keys_words[0].bitcast(I32))
+        nc.sync.dma_start(out=q_raw[1][:], in_=query2.rearrange("(p j) w -> p j w", j=PACK))
+        nc.sync.dma_start(lists[0][:], offs)
+        nc.sync.dma_start(lists[1][:], offs2)
+        nc.sync.dma_start(lists[2][:], offs3)
+        nc.sync.dma_start(lists[3][:], offs4)
+        gain_sb = sb("gain_sb", [P, I])
+        old_sb = sb("old_sb", [P, T])
+        nc.sync.dma_start(out=gain_sb[:], in_=gainm)
+        nc.sync.dma_start(out=old_sb[:], in_=old)
+        lam_sb = sb("lam_sb", [P, 1])
+        damp_sb = sb("damp_sb", [P, 1])
+        nc.gpsimd.dma_start(out=lam_sb[:], in_=lam)
+        nc.gpsimd.dma_start(out=damp_sb[:], in_=damp)
+
+        placed = sb("placed", [P, T])
+        nc.vector.memset(placed[:], 0.0)
+
+        is_pos = sb("is_pos", [P, 1])
+        lam_sign = sb("lam_sign", [P, 1])
+        neg_abs_lam = sb("neg_abs_lam", [P, 1])
+        damp_rows = sb("damp_rows", [P, 1])
+        nc.gpsimd.tensor_scalar(is_pos[:], lam_sb[:], 0.0, None, ALU.is_ge)
+        nc.gpsimd.tensor_scalar(lam_sign[:], is_pos[:], 2.0, -1.0, ALU.mult, ALU.add)
+        nc.gpsimd.tensor_scalar(neg_abs_lam[:], lam_sb[:], lam_sign[:], -1.0, ALU.mult, ALU.mult)
+        nc.gpsimd.tensor_scalar(damp_rows[:], damp_sb[:], float(I), 0.0, ALU.mult, ALU.add)
+
+        q_bf = [sb("q_bf%d" % j, [P, Q, PACK], BF16) for j in range(2)]
+        q_codes = [sb("q_codes%d" % j, [P, Q], U32) for j in range(2)]
+        q_scales = [sb("q_scales%d" % j, [P, Q], U8) for j in range(2)]
+        widths = (256, 512)
+        banks = [[psum.tile([P, widths[j]], F32, name="bank%d%d" % (j, n)) for n in range(T // widths[j])] for j in range(2)]
+        for j in range(2):
+            nc.vector.tensor_copy(out=q_bf[j][:], in_=q_raw[j][:].rearrange("p j w -> p w j"))
+            nc.vector.quantize_mx(
+                out=q_codes[j][:].bitcast(FP8X4), scales=q_scales[j][:], in_=q_bf[j][:].rearrange("p w j -> p (w j)")
+            )
+            w = widths[j]
+            for n in range(T // w):
+                nc.tensor.matmul_mx(
+                    out=banks[j][n][:],
+                    lhsT=q_codes[j][:].bitcast(FP8X4),
+                    lhsT_scale=q_scales[j][:],
+                    rhs=key_words[:, 2 * w * n : 2 * w * (n + 1)].bitcast(FP4X4),
+                    rhs_scale=key_scales[:, w * n : w * (n + 1)],
+                    start=True,
+                    stop=True,
+                )
+        a_sb = sb("a_sb", [P, T])
+        b_sb = sb("b_sb", [P, T])
+        for n in range(4):
+            cols = slice(256 * n, 256 * (n + 1))
+            if n < 3:
+                nc.scalar.copy(out=a_sb[:, cols], in_=banks[0][n][:])
+            else:
+                nc.vector.tensor_copy(out=a_sb[:, cols], in_=banks[0][n][:])
+
+        def picked(window, j, h):
+            return window[:].indirect(lists[j][:, LCOL * h : LCOL * (h + 1)])
+
+        def halves(name):
+            return [sb("%s%d" % (name, h), [P, HALF]) for h in range(2)]
+
+        a1 = halves("a1")
+        d = [sb("d%d" % h, [P, 2 * HALF]) for h in range(2)]
+        e = [sb("e%d" % h, [P, 2 * HALF]) for h in range(2)]
+        nc.scalar.activation(a1[0][:], picked(a_sb, 0, 0), ACT.Copy)
+        nc.vector.tensor_copy(a1[1][:], picked(a_sb, 0, 1))
+        for n in range(2):
+            nc.scalar.copy(out=b_sb[:, BANK * n : BANK * (n + 1)], in_=banks[1][n][:])
+        for h in range(2):
+            nc.vector.tensor_tensor(d[h][:, :HALF], picked(a_sb, 1, h), a1[h][:], ALU.subtract)
+        b3 = sb("b3", [P, HALF])
+        nc.scalar.activation(b3[:], picked(b_sb, 2, 1), ACT.Copy)
+        nc.vector.tensor_tensor(d[0][:, HALF:], picked(b_sb, 2, 0), a1[0][:], ALU.subtract)
+        nc.vector.tensor_tensor(d[1][:, HALF:], b3[:], a1[1][:], ALU.subtract)
+        for h in range(2):
+            nc.scalar.activation(e[h][:], d[h][:], ACT.Exp)
+
+        part, f = halves("part"), halves("f")
+        den = sb("den", [P, I])
+        signed = sb("signed", [P, I])
+        for h in range(2):
+            nc.vector.tensor_scalar(part[h][:], e[h][:, :HALF], CAP, 1.0, ALU.min, ALU.add)
+            nc.vector.scalar_tensor_tensor(den[:, HALF * h : HALF * (h + 1)], e[h][:, HALF:], CAP, part[h][:], ALU.min, ALU.add)
+
+        H2, H4 = HALF // 2, HALF // 4
+        pair = [sb("pair%d" % h, [P, H2]) for h in range(2)]
+        quad = [sb("quad%d" % h, [P, H4]) for h in range(2)]
+        rquad = [sb("rquad%d" % h, [P, H4]) for h in range(2)]
+        rpair = [sb("rpair%d" % h, [P, H2]) for h in range(2)]
+        lo = [den[:, HALF * h : HALF * h + H2] for h in range(2)]
+        hi = [den[:, HALF * h + H2 : HALF * (h + 1)] for h in range(2)]
+        extreme = [sb("extreme%d" % h, [P, 1]) for h in range(2)]
+        rext = sb("rext", [P, 1])
+        shift = sb("shift", [P, 1])
+
+        def two(ap):
+            return ap.rearrange("p (s c) -> p s c", s=2)
+
+        for h in range(2):
+            nc.vector.tensor_tensor(pair[h][:], lo[h], hi[h], ALU.mult)
+        nc.vector.tensor_scalar(signed[:, :HALF], den[:, :HALF], lam_sign[:], None, ALU.mult, ALU.min, accum_out=extreme[0][:])
+        for h in range(2):
+            nc.vector.tensor_tensor(quad[h][:], pair[h][:, :H4], pair[h][:, H4:], ALU.mult)
+        nc.vector.tensor_scalar(signed[:, HALF:], den[:, HALF:], lam_sign[:], extreme[0][:], ALU.mult, ALU.min, accum_out=extreme[1][:])
+        nc.vector.reciprocal(rquad[0][:], quad[0][:])
+        nc.vector.reciprocal(rext[:], extreme[1][:])
+        nc.vector.reciprocal(rquad[1][:], quad[1][:])
+        nc.vector.tensor_tensor(shift[:], rext[:], neg_abs_lam[:], ALU.mult)
+        for h in range(2):
+            nc.vector.tensor_tensor(
+                two(rpair[h][:]), two(pair[h][:])[:, ::-1, :], rquad[h][:].unsqueeze(1).to_broadcast([P, 2, H4]), ALU.mult
+            )
+        p = sb("p", [P, I])
+        psum_h = [sb("p_sum%d" % h, [P, 1]) for h in range(2)]
+        for h in range(2):
+            cols = slice(HALF * h, HALF * (h + 1))
+            nc.vector.tensor_tensor(
+                two(f[h][:]), two(den[:, cols])[:, ::-1, :], rpair[h][:].unsqueeze(1).to_broadcast([P, 2, H2]), ALU.mult
+            )
+            nc.scalar.activation(p[:, cols], f[h][:], ACT.Exp, bias=shift[:], scale=lam_sb[:], accum_out=psum_h[h][:])
+
+        p_total = sb("p_total", [P, 1])
+        r_p = sb("r_p", [P, 1])
+        ln_scale = sb("ln_scale", [P, 1])
+        nc.vector.tensor_tensor(p_total[:], psum_h[0][:], psum_h[1][:], ALU.add)
+        nc.vector.reciprocal(r_p[:], p_total[:])
+        nc.vector.tensor_tensor(ln_scale[:], r_p[:], damp_rows[:], ALU.mult)
+
+        cuts = (slice(0, 128), slice(128, I))
+        u0 = [sb("u0%d" % h, [P, c.stop - c.start]) for h, c in enumerate(cuts)]
+        usum_h = [sb("u_sum%d" % h, [P, 1]) for h in range(2)]
+        u_total = sb("u_total", [P, 1])
+        r_u = sb("r_u", [P, 1])
+        for h, c in enumerate(cuts):
+            nc.scalar.activation(u0[h][:], p[:, c], ACT.Ln, bias=1.0, scale=ln_scale[:], accum_out=usum_h[h][:])
+
+        def scatter(h):
+            c = cuts[h]
+            nc.vector.tensor_tensor(placed[:].indirect(lists[3][:, c.start // 16 : c.stop // 16]), u0[h][:], gain_sb[:, c], ALU.mult)
+
+        scatter(0)
+        nc.vector.tensor_scalar(u_total[:], usum_h[0][:], usum_h[1][:], 1.0 / I, ALU.add, ALU.mult)
+        scatter(1)
+        nc.vector.reciprocal(r_u[:], u_total[:])
+
+        result = sb("result", [P, T])
+        W = T // 4
+        for c in range(4):
+            cols = slice(W * c, W * (c + 1))
+            nc.vector.scalar_tensor_tensor(result[:, cols], placed[:, cols], r_u[:], old_sb[:, cols], ALU.mult, ALU.add)
+            queue = nc.sync if c % 2 == 0 else nc.scalar
+            queue.dma_start(out=out[:, cols], in_=result[:, cols])

@@ -37,14 +37,14 @@ def tile_attend_quotaratio_dampened_moved_heads_kernel(
 
         key_scales = sb("key_scales", [P, T], U8)
         nc.vector.memset(key_scales[:].bitcast(I32), 0)
-        for g in range(4):
-            nc.scalar.dma_start(
-                out=key_scales[32 * g : 32 * g + 4, :].bitcast(I32), in_=keys_scales[0, 4 * g : 4 * g + 4, :].bitcast(I32)
-            )
         q_raw = [sb("q_raw%d" % j, [P, PACK, Q]) for j in range(2)]
         key_words = sb("key_words", [P, 2 * T], U8)
         lists = [keep.tile([P, I // 16], U16, name="list%d" % j) for j in range(4)]
         nc.sync.dma_start(out=q_raw[0][:], in_=query.rearrange("(p j) w -> p j w", j=PACK))
+        for g in range(4):
+            nc.sync.dma_start(
+                out=key_scales[32 * g : 32 * g + 4, :].bitcast(I32), in_=keys_scales[0, 4 * g : 4 * g + 4, :].bitcast(I32)
+            )
         nc.sync.dma_start(out=key_words[:].bitcast(I32), in_=keys_words[0].bitcast(I32))
         nc.sync.dma_start(out=q_raw[1][:], in_=query2.rearrange("(p j) w -> p j w", j=PACK))
         nc.sync.dma_start(lists[0][:], offs)
@@ -67,15 +67,17 @@ def tile_attend_quotaratio_dampened_moved_heads_kernel(
         lam_sign = sb("lam_sign", [P, 1])
         neg_abs_lam = sb("neg_abs_lam", [P, 1])
         damp_rows = sb("damp_rows", [P, 1])
+        abs_lam = sb("abs_lam", [P, 1])
         nc.gpsimd.tensor_scalar(is_pos[:], lam_sb[:], 0.0, None, ALU.is_ge)
         nc.gpsimd.tensor_scalar(lam_sign[:], is_pos[:], 2.0, -1.0, ALU.mult, ALU.add)
         nc.gpsimd.tensor_scalar(neg_abs_lam[:], lam_sb[:], lam_sign[:], -1.0, ALU.mult, ALU.mult)
+        nc.gpsimd.tensor_scalar(abs_lam[:], lam_sb[:], lam_sign[:], 0.0, ALU.mult, ALU.add)
         nc.gpsimd.tensor_scalar(damp_rows[:], damp_sb[:], float(I), 0.0, ALU.mult, ALU.add)
 
         q_bf = [sb("q_bf%d" % j, [P, Q, PACK], BF16) for j in range(2)]
         q_codes = [sb("q_codes%d" % j, [P, Q], U32) for j in range(2)]
         q_scales = [sb("q_scales%d" % j, [P, Q], U8) for j in range(2)]
-        widths = (256, 512)
+        widths = (256, 256)
         banks = [[psum.tile([P, widths[j]], F32, name="bank%d%d" % (j, n)) for n in range(T // widths[j])] for j in range(2)]
         for j in range(2):
             nc.vector.tensor_copy(out=q_bf[j][:], in_=q_raw[j][:].rearrange("p j w -> p w j"))
@@ -97,10 +99,8 @@ def tile_attend_quotaratio_dampened_moved_heads_kernel(
         b_sb = sb("b_sb", [P, T])
         for n in range(4):
             cols = slice(256 * n, 256 * (n + 1))
-            if n < 3:
-                nc.scalar.copy(out=a_sb[:, cols], in_=banks[0][n][:])
-            else:
-                nc.vector.tensor_copy(out=a_sb[:, cols], in_=banks[0][n][:])
+            nc.scalar.copy(out=a_sb[:, cols], in_=banks[0][n][:])
+        nc.vector.tensor_copy(out=b_sb[:, :256], in_=banks[1][0][:])
 
         def picked(window, j, h):
             return window[:].indirect(lists[j][:, LCOL * h : LCOL * (h + 1)])
@@ -111,53 +111,48 @@ def tile_attend_quotaratio_dampened_moved_heads_kernel(
         a1 = halves("a1")
         d = [sb("d%d" % h, [P, 2 * HALF]) for h in range(2)]
         e = [sb("e%d" % h, [P, 2 * HALF]) for h in range(2)]
-        nc.scalar.activation(a1[0][:], picked(a_sb, 0, 0), ACT.Copy)
-        nc.vector.tensor_copy(a1[1][:], picked(a_sb, 0, 1))
-        for n in range(2):
-            nc.scalar.copy(out=b_sb[:, BANK * n : BANK * (n + 1)], in_=banks[1][n][:])
-        for h in range(2):
-            nc.vector.tensor_tensor(d[h][:, :HALF], picked(a_sb, 1, h), a1[h][:], ALU.subtract)
+        nc.vector.tensor_copy(a1[0][:], picked(a_sb, 0, 0))
+        for n in range(1, 4):
+            nc.scalar.copy(out=b_sb[:, 256 * n : 256 * (n + 1)], in_=banks[1][n][:])
+        nc.scalar.activation(a1[1][:], picked(a_sb, 0, 1), ACT.Copy)
+        nc.vector.tensor_tensor(d[0][:, :HALF], picked(a_sb, 1, 0), a1[0][:], ALU.subtract)
         b3 = sb("b3", [P, HALF])
         nc.scalar.activation(b3[:], picked(b_sb, 2, 1), ACT.Copy)
         nc.vector.tensor_tensor(d[0][:, HALF:], picked(b_sb, 2, 0), a1[0][:], ALU.subtract)
+        nc.vector.tensor_tensor(d[1][:, :HALF], picked(a_sb, 1, 1), a1[1][:], ALU.subtract)
         nc.vector.tensor_tensor(d[1][:, HALF:], b3[:], a1[1][:], ALU.subtract)
         for h in range(2):
             nc.scalar.activation(e[h][:], d[h][:], ACT.Exp)
 
-        part, f = halves("part"), halves("f")
+        total, f = halves("total"), halves("f")
         den = sb("den", [P, I])
-        signed = sb("signed", [P, I])
         for h in range(2):
-            nc.vector.tensor_scalar(part[h][:], e[h][:, :HALF], CAP, 1.0, ALU.min, ALU.add)
-            nc.vector.scalar_tensor_tensor(den[:, HALF * h : HALF * (h + 1)], e[h][:, HALF:], CAP, part[h][:], ALU.min, ALU.add)
+            nc.vector.scalar_tensor_tensor(total[h][:], e[h][:, :HALF], 1.0, e[h][:, HALF:], ALU.add, ALU.add)
+            nc.vector.tensor_scalar(den[:, HALF * h : HALF * (h + 1)], total[h][:], CAP, lam_sign[:], ALU.min, ALU.mult)
 
         H2, H4 = HALF // 2, HALF // 4
-        pair = [sb("pair%d" % h, [P, H2]) for h in range(2)]
-        quad = [sb("quad%d" % h, [P, H4]) for h in range(2)]
+        pair = sb("pair", [P, 2, H2])
+        quad = sb("quad", [P, 2, H4])
         rquad = [sb("rquad%d" % h, [P, H4]) for h in range(2)]
         rpair = [sb("rpair%d" % h, [P, H2]) for h in range(2)]
-        lo = [den[:, HALF * h : HALF * h + H2] for h in range(2)]
-        hi = [den[:, HALF * h + H2 : HALF * (h + 1)] for h in range(2)]
-        extreme = [sb("extreme%d" % h, [P, 1]) for h in range(2)]
+        extreme = sb("extreme", [P, 1])
         rext = sb("rext", [P, 1])
         shift = sb("shift", [P, 1])
 
         def two(ap):
             return ap.rearrange("p (s c) -> p s c", s=2)
 
+        den4 = den[:].rearrange("p (h s c) -> p h s c", h=2, s=2)
+        nc.vector.tensor_tensor(pair[:], den4[:, :, 0, :], den4[:, :, 1, :], ALU.mult)
+        nc.vector.tensor_reduce(extreme[:], den[:], mybir.AxisListType.X, ALU.min)
+        nc.vector.tensor_tensor(quad[:], pair[:, :, :H4], pair[:, :, H4:], ALU.mult)
+        nc.vector.reciprocal(rext[:], extreme[:])
         for h in range(2):
-            nc.vector.tensor_tensor(pair[h][:], lo[h], hi[h], ALU.mult)
-        nc.vector.tensor_scalar(signed[:, :HALF], den[:, :HALF], lam_sign[:], None, ALU.mult, ALU.min, accum_out=extreme[0][:])
-        for h in range(2):
-            nc.vector.tensor_tensor(quad[h][:], pair[h][:, :H4], pair[h][:, H4:], ALU.mult)
-        nc.vector.tensor_scalar(signed[:, HALF:], den[:, HALF:], lam_sign[:], extreme[0][:], ALU.mult, ALU.min, accum_out=extreme[1][:])
-        nc.vector.reciprocal(rquad[0][:], quad[0][:])
-        nc.vector.reciprocal(rext[:], extreme[1][:])
-        nc.vector.reciprocal(rquad[1][:], quad[1][:])
+            nc.vector.reciprocal(rquad[h][:], quad[:, h, :])
         nc.vector.tensor_tensor(shift[:], rext[:], neg_abs_lam[:], ALU.mult)
         for h in range(2):
             nc.vector.tensor_tensor(
-                two(rpair[h][:]), two(pair[h][:])[:, ::-1, :], rquad[h][:].unsqueeze(1).to_broadcast([P, 2, H4]), ALU.mult
+                two(rpair[h][:]), two(pair[:, h, :])[:, ::-1, :], rquad[h][:].unsqueeze(1).to_broadcast([P, 2, H4]), ALU.mult
             )
         p = sb("p", [P, I])
         psum_h = [sb("p_sum%d" % h, [P, 1]) for h in range(2)]
@@ -166,7 +161,7 @@ def tile_attend_quotaratio_dampened_moved_heads_kernel(
             nc.vector.tensor_tensor(
                 two(f[h][:]), two(den[:, cols])[:, ::-1, :], rpair[h][:].unsqueeze(1).to_broadcast([P, 2, H2]), ALU.mult
             )
-            nc.scalar.activation(p[:, cols], f[h][:], ACT.Exp, bias=shift[:], scale=lam_sb[:], accum_out=psum_h[h][:])
+            nc.scalar.activation(p[:, cols], f[h][:], ACT.Exp, bias=shift[:], scale=abs_lam[:], accum_out=psum_h[h][:])
 
         p_total = sb("p_total", [P, 1])
         r_p = sb("r_p", [P, 1])
@@ -193,9 +188,9 @@ def tile_attend_quotaratio_dampened_moved_heads_kernel(
         nc.vector.reciprocal(r_u[:], u_total[:])
 
         result = sb("result", [P, T])
-        W = T // 4
+        edges = (0, 320, 640, 896, T)
         for c in range(4):
-            cols = slice(W * c, W * (c + 1))
+            cols = slice(edges[c], edges[c + 1])
             nc.vector.scalar_tensor_tensor(result[:, cols], placed[:, cols], r_u[:], old_sb[:, cols], ALU.mult, ALU.add)
             queue = nc.sync if c % 2 == 0 else nc.scalar
             queue.dma_start(out=out[:, cols], in_=result[:, cols])

@@ -58,21 +58,15 @@ def tile_attend_quotaratio_dampened_moved_heads_kernel(
         lam_sb = sb("lam_sb", [P, 1])
         damp_sb = sb("damp_sb", [P, 1])
         nc.gpsimd.dma_start(out=lam_sb[:], in_=lam)
-        nc.gpsimd.dma_start(out=damp_sb[:], in_=damp)
+        nc.sync.dma_start(out=damp_sb[:], in_=damp)
 
         placed = sb("placed", [P, T])
         nc.vector.memset(placed[:], 0.0)
 
-        is_pos = sb("is_pos", [P, 1])
-        lam_sign = sb("lam_sign", [P, 1])
-        neg_abs_lam = sb("neg_abs_lam", [P, 1])
-        damp_rows = sb("damp_rows", [P, 1])
-        abs_lam = sb("abs_lam", [P, 1])
-        nc.gpsimd.tensor_scalar(is_pos[:], lam_sb[:], 0.0, None, ALU.is_ge)
-        nc.gpsimd.tensor_scalar(lam_sign[:], is_pos[:], 2.0, -1.0, ALU.mult, ALU.add)
-        nc.gpsimd.tensor_scalar(neg_abs_lam[:], lam_sb[:], lam_sign[:], -1.0, ALU.mult, ALU.mult)
-        nc.gpsimd.tensor_scalar(abs_lam[:], lam_sb[:], lam_sign[:], 0.0, ALU.mult, ALU.add)
-        nc.gpsimd.tensor_scalar(damp_rows[:], damp_sb[:], float(I), 0.0, ALU.mult, ALU.add)
+        half_sign = sb("half_sign", [P, 1])
+        exp_scale = sb("exp_scale", [P, 1])
+        nc.gpsimd.tensor_scalar(half_sign[:], lam_sb[:], 0.0, 0.5, ALU.is_ge, ALU.subtract)
+        nc.gpsimd.tensor_tensor(exp_scale[:], lam_sb[:], half_sign[:], ALU.mult)
 
         q_bf = [sb("q_bf%d" % j, [P, Q, PACK], BF16) for j in range(2)]
         q_codes = [sb("q_codes%d" % j, [P, Q], U32) for j in range(2)]
@@ -125,50 +119,75 @@ def tile_attend_quotaratio_dampened_moved_heads_kernel(
             nc.scalar.activation(e[h][:], d[h][:], ACT.Exp)
 
         total, f = halves("total"), halves("f")
-        den = sb("den", [P, I])
-        for h in range(2):
-            nc.vector.scalar_tensor_tensor(total[h][:], e[h][:, :HALF], 1.0, e[h][:, HALF:], ALU.add, ALU.add)
-            nc.vector.tensor_scalar(den[:, HALF * h : HALF * (h + 1)], total[h][:], CAP, lam_sign[:], ALU.min, ALU.mult)
-
+        den = sb("den", [P, I + 1])
         H2, H4 = HALF // 2, HALF // 4
-        pair = sb("pair", [P, 2, H2])
-        quad = sb("quad", [P, 2, H4])
+        pair = [sb("pair%d" % h, [P, H2]) for h in range(2)]
+        quad = [sb("quad%d" % h, [P, H4]) for h in range(2)]
         rquad = [sb("rquad%d" % h, [P, H4]) for h in range(2)]
         rpair = [sb("rpair%d" % h, [P, H2]) for h in range(2)]
         extreme = sb("extreme", [P, 1])
         rext = sb("rext", [P, 1])
         shift = sb("shift", [P, 1])
+        p = sb("p", [P, I])
+        psum_h = [sb("p_sum%d" % h, [P, 1]) for h in range(2)]
+        slots = [slice(HALF * h, HALF * (h + 1)) for h in range(2)]
 
         def two(ap):
             return ap.rearrange("p (s c) -> p s c", s=2)
 
-        den4 = den[:].rearrange("p (h s c) -> p h s c", h=2, s=2)
-        nc.vector.tensor_tensor(pair[:], den4[:, :, 0, :], den4[:, :, 1, :], ALU.mult)
-        nc.vector.tensor_reduce(extreme[:], den[:], mybir.AxisListType.X, ALU.min)
-        nc.vector.tensor_tensor(quad[:], pair[:, :, :H4], pair[:, :, H4:], ALU.mult)
+        def add_up(h):
+            nc.vector.scalar_tensor_tensor(total[h][:], e[h][:, :HALF], 1.0, e[h][:, HALF:], ALU.add, ALU.add)
+
+        def cap(h):
+            nc.vector.tensor_scalar(den[:, slots[h]], total[h][:], CAP, half_sign[:], ALU.min, ALU.mult)
+
+        def pairs(h):
+            both = two(den[:, slots[h]])
+            nc.vector.tensor_tensor(pair[h][:], both[:, 0, :], both[:, 1, :], ALU.mult)
+
+        def quads(h):
+            nc.vector.tensor_tensor(quad[h][:], pair[h][:, :H4], pair[h][:, H4:], ALU.mult)
+
+        def invert(h):
+            nc.vector.reciprocal(rquad[h][:], quad[h][:])
+
+        def unpair(h):
+            nc.vector.tensor_tensor(
+                two(rpair[h][:]), two(pair[h][:])[:, ::-1, :], rquad[h][:].unsqueeze(1).to_broadcast([P, 2, H4]), ALU.mult
+            )
+
+        def single(h):
+            nc.vector.tensor_tensor(
+                two(f[h][:]), two(den[:, slots[h]])[:, ::-1, :], rpair[h][:].unsqueeze(1).to_broadcast([P, 2, H2]), ALU.mult
+            )
+
+        add_up(0)
+        cap(0)
+        pairs(0)
+        nc.vector.tensor_reduce(den[:, I : I + 1], den[:, slots[0]], mybir.AxisListType.X, ALU.min)
+        quads(0)
+        add_up(1)
+        invert(0)
+        cap(1)
+        unpair(0)
+        pairs(1)
+        single(0)
+        quads(1)
+        nc.vector.tensor_reduce(extreme[:], den[:, HALF : I + 1], mybir.AxisListType.X, ALU.min)
+        invert(1)
         nc.vector.reciprocal(rext[:], extreme[:])
+        unpair(1)
+        nc.vector.tensor_scalar(shift[:], rext[:], exp_scale[:], -1.0, ALU.mult, ALU.mult)
+        single(1)
         for h in range(2):
-            nc.vector.reciprocal(rquad[h][:], quad[:, h, :])
-        nc.vector.tensor_tensor(shift[:], rext[:], neg_abs_lam[:], ALU.mult)
-        for h in range(2):
-            nc.vector.tensor_tensor(
-                two(rpair[h][:]), two(pair[:, h, :])[:, ::-1, :], rquad[h][:].unsqueeze(1).to_broadcast([P, 2, H4]), ALU.mult
-            )
-        p = sb("p", [P, I])
-        psum_h = [sb("p_sum%d" % h, [P, 1]) for h in range(2)]
-        for h in range(2):
-            cols = slice(HALF * h, HALF * (h + 1))
-            nc.vector.tensor_tensor(
-                two(f[h][:]), two(den[:, cols])[:, ::-1, :], rpair[h][:].unsqueeze(1).to_broadcast([P, 2, H2]), ALU.mult
-            )
-            nc.scalar.activation(p[:, cols], f[h][:], ACT.Exp, bias=shift[:], scale=abs_lam[:], accum_out=psum_h[h][:])
+            nc.scalar.activation(p[:, slots[h]], f[h][:], ACT.Exp, bias=shift[:], scale=exp_scale[:], accum_out=psum_h[h][:])
 
         p_total = sb("p_total", [P, 1])
         r_p = sb("r_p", [P, 1])
         ln_scale = sb("ln_scale", [P, 1])
         nc.vector.tensor_tensor(p_total[:], psum_h[0][:], psum_h[1][:], ALU.add)
         nc.vector.reciprocal(r_p[:], p_total[:])
-        nc.vector.tensor_tensor(ln_scale[:], r_p[:], damp_rows[:], ALU.mult)
+        nc.vector.tensor_scalar(ln_scale[:], r_p[:], damp_sb[:], float(I), ALU.mult, ALU.mult)
 
         cuts = (slice(0, 128), slice(128, I))
         u0 = [sb("u0%d" % h, [P, c.stop - c.start]) for h, c in enumerate(cuts)]

@@ -94,7 +94,6 @@ def tile_attend_quotaratio_dampened_moved_heads_kernel(
         for n in range(4):
             cols = slice(256 * n, 256 * (n + 1))
             nc.scalar.copy(out=a_sb[:, cols], in_=banks[0][n][:])
-        nc.vector.tensor_copy(out=b_sb[:, :256], in_=banks[1][0][:])
 
         def picked(window, j, h):
             return window[:].indirect(lists[j][:, LCOL * h : LCOL * (h + 1)])
@@ -106,7 +105,7 @@ def tile_attend_quotaratio_dampened_moved_heads_kernel(
         d = [sb("d%d" % h, [P, 2 * HALF]) for h in range(2)]
         e = [sb("e%d" % h, [P, 2 * HALF]) for h in range(2)]
         nc.vector.tensor_copy(a1[0][:], picked(a_sb, 0, 0))
-        for n in range(1, 4):
+        for n in range(4):
             nc.scalar.copy(out=b_sb[:, 256 * n : 256 * (n + 1)], in_=banks[1][n][:])
         nc.scalar.activation(a1[1][:], picked(a_sb, 0, 1), ACT.Copy)
         nc.vector.tensor_tensor(d[0][:, :HALF], picked(a_sb, 1, 0), a1[0][:], ALU.subtract)

from contextlib import ExitStack

import concourse.mybir as mybir

D, T, I, Q = 512, 1024, 512, 128
FLOPS = 2 * 2 * D * T * Q

F32 = mybir.dt.float32
BF16 = mybir.dt.bfloat16
I32 = mybir.dt.int32
U32 = mybir.dt.uint32
U16 = mybir.dt.uint16
U8 = mybir.dt.uint8
FP8X4 = mybir.dt.float8_e4m3fn_x4
FP4X4 = mybir.dt.float4_e2m1fn_x4
ALU = mybir.AluOpType
ACT = mybir.ActivationFunctionType

P = 128
PACK = 4
BANK = 512
HALF = I // 2
LCOL = HALF // 16
CAP = float(2 ** 30)


def tile_attend_quotaratio_dampened_moved_heads_kernel(
    tc, query, query2, keys_words, keys_scales, lam, damp, old, gainm, offs, offs2, offs3, offs4, out
):
    nc = tc.nc
    with ExitStack() as ctx:
        keep = ctx.enter_context(tc.tile_pool(name="keep", bufs=1))
        psum = ctx.enter_context(tc.psum_pool(name="psum", bufs=1))

        def sb(name, shape, dtype=F32):
            return keep.tile(shape, dtype, name=name, align_bytes=64)

        key_scales = sb("key_scales", [P, T], U8)
        nc.vector.memset(key_scales[:].bitcast(I32), 0)
        q_raw = [sb("q_raw%d" % j, [P, PACK, Q]) for j in range(2)]
        key_words = sb("key_words", [P, 2 * T], U8)
        lists = [keep.tile([P, I // 16], U16, name="list%d" % j) for j in range(4)]
        nc.sync.dma_start(out=q_raw[0][:], in_=query.rearrange("(p j) w -> p j w", j=PACK))
        for g in range(4):
            nc.sync.dma_start(
                out=key_scales[32 * g : 32 * g + 4, :].bitcast(I32), in_=keys_scales[0, 4 * g : 4 * g + 4, :].bitcast(I32)
            )
        nc.sync.dma_start(out=key_words[:].bitcast(I32), in_=keys_words[0].bitcast(I32))
        nc.sync.dma_start(out=q_raw[1][:], in_=query2.rearrange("(p j) w -> p j w", j=PACK))
        nc.sync.dma_start(lists[0][:], offs)
        nc.sync.dma_start(lists[1][:], offs2)
        nc.sync.dma_start(lists[2][:], offs3)
        nc.sync.dma_start(lists[3][:], offs4)
        gain_sb = sb("gain_sb", [P, I])
        old_sb = sb("old_sb", [P, T])
        nc.sync.dma_start(out=gain_sb[:], in_=gainm)
        nc.sync.dma_start(out=old_sb[:], in_=old)
        lam_sb = sb("lam_sb", [P, 1])
        damp_sb = sb("damp_sb", [P, 1])
        nc.gpsimd.dma_start(out=lam_sb[:], in_=lam)
        nc.sync.dma_start(out=damp_sb[:], in_=damp)

        placed = sb("placed", [P, T])
        nc.vector.memset(placed[:], 0.0)

        half_sign = sb("half_sign", [P, 1])
        exp_scale = sb("exp_scale", [P, 1])
        nc.gpsimd.tensor_scalar(half_sign[:], lam_sb[:], 0.0, 0.5, ALU.is_ge, ALU.subtract)
        nc.gpsimd.tensor_tensor(exp_scale[:], lam_sb[:], half_sign[:], ALU.mult)

        q_bf = [sb("q_bf%d" % j, [P, Q, PACK], BF16) for j in range(2)]
        q_codes = [sb("q_codes%d" % j, [P, Q], U32) for j in range(2)]
        q_scales = [sb("q_scales%d" % j, [P, Q], U8) for j in range(2)]
        widths = (256, 256)
        banks = [[psum.tile([P, widths[j]], F32, name="bank%d%d" % (j, n)) for n in range(T // widths[j])] for j in range(2)]
        for j in range(2):
            nc.vector.tensor_copy(out=q_bf[j][:], in_=q_raw[j][:].rearrange("p j w -> p w j"))
            nc.vector.quantize_mx(
                out=q_codes[j][:].bitcast(FP8X4), scales=q_scales[j][:], in_=q_bf[j][:].rearrange("p w j -> p (w j)")
            )
            w = widths[j]
            for n in range(T // w):
                nc.tensor.matmul_mx(
                    out=banks[j][n][:],
                    lhsT=q_codes[j][:].bitcast(FP8X4),
                    lhsT_scale=q_scales[j][:],
                    rhs=key_words[:, 2 * w * n : 2 * w * (n + 1)].bitcast(FP4X4),
                    rhs_scale=key_scales[:, w * n : w * (n + 1)],
                    start=True,
                    stop=True,
                )
        a_sb = sb("a_sb", [P, T])
        b_sb = sb("b_sb", [P, T])
        for n in range(4):
            cols = slice(256 * n, 256 * (n + 1))
            nc.scalar.copy(out=a_sb[:, cols], in_=banks[0][n][:])

        def picked(window, j, h):
            return window[:].indirect(lists[j][:, LCOL * h : LCOL * (h + 1)])

        def halves(name):
            return [sb("%s%d" % (name, h), [P, HALF]) for h in range(2)]

        a1 = halves("a1")
        d = [sb("d%d" % h, [P, 2 * HALF]) for h in range(2)]
        e = [sb("e%d" % h, [P, 2 * HALF]) for h in range(2)]
        nc.vector.tensor_copy(a1[0][:], picked(a_sb, 0, 0))
        for n in range(4):
            nc.scalar.copy(out=b_sb[:, 256 * n : 256 * (n + 1)], in_=banks[1][n][:])
        nc.scalar.activation(a1[1][:], picked(a_sb, 0, 1), ACT.Copy)
        nc.vector.tensor_tensor(d[0][:, :HALF], picked(a_sb, 1, 0), a1[0][:], ALU.subtract)
        b3 = sb("b3", [P, HALF])
        nc.scalar.activation(b3[:], picked(b_sb, 2, 1), ACT.Copy)
        nc.vector.tensor_tensor(d[0][:, HALF:], picked(b_sb, 2, 0), a1[0][:], ALU.subtract)
        nc.vector.tensor_tensor(d[1][:, :HALF], picked(a_sb, 1, 1), a1[1][:], ALU.subtract)
        nc.vector.tensor_tensor(d[1][:, HALF:], b3[:], a1[1][:], ALU.subtract)
        for h in range(2):
            nc.scalar.activation(e[h][:], d[h][:], ACT.Exp)

        total, f = halves("total"), halves("f")
        den = sb("den", [P, I + 1])
        H2, H4 = HALF // 2, HALF // 4
        pair = [sb("pair%d" % h, [P, H2]) for h in range(2)]
        quad = [sb("quad%d" % h, [P, H4]) for h in range(2)]
        rquad = [sb("rquad%d" % h, [P, H4]) for h in range(2)]
        rpair = [sb("rpair%d" % h, [P, H2]) for h in range(2)]
        extreme = sb("extreme", [P, 1])
        rext = sb("rext", [P, 1])
        shift = sb("shift", [P, 1])
        p = sb("p", [P, I])
        psum_h = [sb("p_sum%d" % h, [P, 1]) for h in range(2)]
        slots = [slice(HALF * h, HALF * (h + 1)) for h in range(2)]

        def two(ap):
            return ap.rearrange("p (s c) -> p s c", s=2)

        def add_up(h):
            nc.vector.scalar_tensor_tensor(total[h][:], e[h][:, :HALF], 1.0, e[h][:, HALF:], ALU.add, ALU.add)

        def cap(h):
            nc.vector.tensor_scalar(den[:, slots[h]], total[h][:], CAP, half_sign[:], ALU.min, ALU.mult)

        def pairs(h):
            both = two(den[:, slots[h]])
            nc.vector.tensor_tensor(pair[h][:], both[:, 0, :], both[:, 1, :], ALU.mult)

        def quads(h):
            nc.vector.tensor_tensor(quad[h][:], pair[h][:, :H4], pair[h][:, H4:], ALU.mult)

        def invert(h):
            nc.vector.reciprocal(rquad[h][:], quad[h][:])

        def unpair(h):
            nc.vector.tensor_tensor(
                two(rpair[h][:]), two(pair[h][:])[:, ::-1, :], rquad[h][:].unsqueeze(1).to_broadcast([P, 2, H4]), ALU.mult
            )

        def single(h):
            nc.vector.tensor_tensor(
                two(f[h][:]), two(den[:, slots[h]])[:, ::-1, :], rpair[h][:].unsqueeze(1).to_broadcast([P, 2, H2]), ALU.mult
            )

        add_up(0)
        cap(0)
        pairs(0)
        nc.vector.tensor_reduce(den[:, I : I + 1], den[:, slots[0]], mybir.AxisListType.X, ALU.min)
        quads(0)
        add_up(1)
        invert(0)
        cap(1)
        unpair(0)
        pairs(1)
        single(0)
        quads(1)
        nc.vector.tensor_reduce(extreme[:], den[:, HALF : I + 1], mybir.AxisListType.X, ALU.min)
        invert(1)
        nc.vector.reciprocal(rext[:], extreme[:])
        unpair(1)
        nc.vector.tensor_scalar(shift[:], rext[:], exp_scale[:], -1.0, ALU.mult, ALU.mult)
        single(1)
        for h in range(2):
            nc.scalar.activation(p[:, slots[h]], f[h][:], ACT.Exp, bias=shift[:], scale=exp_scale[:], accum_out=psum_h[h][:])

        p_total = sb("p_total", [P, 1])
        r_p = sb("r_p", [P, 1])
        ln_scale = sb("ln_scale", [P, 1])
        nc.vector.tensor_tensor(p_total[:], psum_h[0][:], psum_h[1][:], ALU.add)
        nc.vector.reciprocal(r_p[:], p_total[:])
        nc.vector.tensor_scalar(ln_scale[:], r_p[:], damp_sb[:], float(I), ALU.mult, ALU.mult)

        cuts = (slice(0, 128), slice(128, I))
        u0 = [sb("u0%d" % h, [P, c.stop - c.start]) for h, c in enumerate(cuts)]
        usum_h = [sb("u_sum%d" % h, [P, 1]) for h in range(2)]
        u_total = sb("u_total", [P, 1])
        r_u = sb("r_u", [P, 1])
        for h, c in enumerate(cuts):
            nc.scalar.activation(u0[h][:], p[:, c], ACT.Ln, bias=1.0, scale=ln_scale[:], accum_out=usum_h[h][:])

        def scatter(h):
            c = cuts[h]
            nc.vector.tensor_tensor(placed[:].indirect(lists[3][:, c.start // 16 : c.stop // 16]), u0[h][:], gain_sb[:, c], ALU.mult)

        scatter(0)
        nc.vector.tensor_scalar(u_total[:], usum_h[0][:], usum_h[1][:], 1.0 / I, ALU.add, ALU.mult)
        scatter(1)
        nc.vector.reciprocal(r_u[:], u_total[:])

        result = sb("result", [P, T])
        edges = (0, 320, 640, 896, T)
        for c in range(4):
            cols = slice(edges[c], edges[c + 1])
            nc.vector.scalar_tensor_tensor(result[:, cols], placed[:, cols], r_u[:], old_sb[:, cols], ALU.mult, ALU.add)
            queue = nc.sync if c % 2 == 0 else nc.scalar
            queue.dma_start(out=out[:, cols], in_=result[:, cols])
